import numpy as np
import ml_dtypes


def mxq(x, axis, fmt="e4m3"):
    dtype, down = {"e4m3": (ml_dtypes.float8_e4m3fn, 7), "e5m2": (ml_dtypes.float8_e5m2, 14)}[fmt]
    v = np.moveaxis(np.asarray(x, np.float32).astype(ml_dtypes.bfloat16).astype(np.float64), axis, -1)
    blocks = v.reshape(v.shape[:-1] + (-1, 32))
    amax = np.abs(blocks).max(-1, keepdims=True)
    byte = np.maximum(np.where(amax > 0, np.frexp(amax)[1] - 1 + 127, 0) - down, 1)
    scale = np.exp2(byte - 127.0)
    codes = (blocks / scale).astype(np.float32).astype(dtype).astype(np.float64)
    return np.moveaxis((codes * scale).reshape(v.shape), -1, axis)


WIDE = False


def mx_kscale(k):
    if not WIDE:
        return np.ones(k)
    levels = np.array([10, -10, 5, -5, 0])
    if k % 512:
        return np.exp2(np.random.permutation(np.resize(levels, k // 32))).repeat(32)
    a = np.empty((k // 512, 16))
    for p in range(k // 512):
        a[p, :8] = np.random.permutation(np.resize(levels, 8))
        for g in range(8):
            far = levels[np.abs(levels - a[p, g]) >= 10]
            a[p, g + 8] = far[np.random.randint(len(far))]
    return np.exp2(a.ravel()).repeat(32)


def f64(x):
    return np.asarray(x).astype(np.float64)


def striped(idx):
    return np.tile(idx.reshape(-1, 16).T, (8, 1)).astype(np.uint16)


def unstriped(offs):
    return offs[:16].T.reshape(-1).astype(np.int64)


def pack_weight(w):
    k, n = w.shape
    w = f64(np.asarray(w, np.float32).astype(ml_dtypes.bfloat16)).reshape(k // 32, 32, n)
    amax = np.abs(w).max(1)
    byte = np.clip(np.where(amax > 0, np.frexp(amax)[1] - 1 + 127 - 7, 1), 1, 254)
    scaled = (w * np.exp2(127.0 - byte)[:, None, :]).reshape(k, n).astype(np.float32)
    words = np.ascontiguousarray(scaled.reshape(k // 512, 128, 4, n).transpose(0, 1, 3, 2)).astype(ml_dtypes.float8_e4m3fn).view(np.uint8)
    return words, np.ascontiguousarray(byte.astype(np.uint8).reshape(k // 512, 16, n))


def unpack_weight(words, scales):
    g, p, n, _ = words.shape
    vals = np.ascontiguousarray(words).view(ml_dtypes.float8_e4m3fn).astype(np.float64) * np.repeat(np.exp2(scales.astype(np.float64) - 127.0), 8, axis=1)[..., None]
    return vals.transpose(0, 1, 3, 2).reshape(g * 512, n)


K, T, S, N = 512, 4096, 1024, 128


def setup_inputs():
    n = np.random.standard_normal
    s = mx_kscale(K)[:, None]
    packed_xT = pack_weight(n((K, T)) * s)
    return {
        "x_words": packed_xT[0],
        "x_scales": packed_xT[1],
        "w1": (n((K, N)) / np.sqrt(K) / s).astype(np.float32),
        "w2": (n((K, N)) / np.sqrt(K) / s).astype(np.float32),
        "w3": (n((K, N)) / np.sqrt(K) / s).astype(np.float32),
        "offs": striped(np.random.permutation(T)[:S]),
    }


def reference(x_words, x_scales, w1, w2, w3, offs):
    xq = unpack_weight(x_words, x_scales)[:, unstriped(offs)]
    return np.maximum(np.maximum(mxq(f64(w1), 0, "e4m3").T @ xq, mxq(f64(w2), 0, "e4m3").T @ xq), mxq(f64(w3), 0, "e4m3").T @ xq)

@@ -1,0 +1,119 @@
+import concourse.mybir as mybir
+
+K, T, S, N = 512, 4096, 1024, 128
+FLOPS = 3 * 2 * K * N * S
+
+F32 = mybir.dt.float32
+BF16 = mybir.dt.bfloat16
+I32 = mybir.dt.int32
+U32 = mybir.dt.uint32
+U16 = mybir.dt.uint16
+U8 = mybir.dt.uint8
+FP8X4 = mybir.dt.float8_e4m3fn_x4
+MAX = mybir.AluOpType.max
+
+P = 128
+PACK = 4
+CHUNK = 512
+PIECE = 256
+
+
+def tile_picked_maxout_max_p_kernel(tc, x_words, x_scales, w1, w2, w3, offs, out):
+    nc = tc.nc
+    with (
+        tc.tile_pool(name="held", bufs=1) as held,
+        tc.tile_pool(name="shared", bufs=1) as shared,
+        tc.psum_pool(name="psum", bufs=1) as psum,
+    ):
+        offsets = held.tile([P, S // 16], U16, name="offsets")
+        nc.sync.dma_start(offsets[:], offs)
+
+        word_table = held.tile([P, T], U32, name="word_table", align_bytes=64)
+        raw = [held.tile([P, PACK, N], F32, name=f"raw{i}", align_bytes=64) for i in range(3)]
+
+        def load_weight(i, w):
+            nc.scalar.dma_start(raw[i][:], w.rearrange("(p t) n -> p t n", t=PACK))
+
+        load_weight(0, w1)
+        nc.scalar.dma_start(word_table[:].bitcast(I32), x_words[0].rearrange("p c t -> p (c t)").bitcast(I32))
+        load_weight(1, w2)
+        load_weight(2, w3)
+
+        table_start = 4 * CHUNK
+        scale_table = shared.tile([P, T], U8, name="scale_table", align_bytes=64, offset=table_start)
+        nc.vector.memset(scale_table[:].bitcast(I32), 0)
+        nc.sync.dma_start(scale_table[0:P:8, :].bitcast(I32), x_scales[0].bitcast(I32))
+        x_plane = held.tile([P, S], U8, name="x_plane", align_bytes=64)
+        nc.vector.memset(x_plane[:].bitcast(I32), 0)
+
+        picked_rows = held.tile([P, S], U8, name="picked_rows", align_bytes=64)
+        nc.vector.tensor_copy(picked_rows[:], scale_table[:].indirect(offsets[:]))
+        for r in range(4):
+            nc.sync.dma_start(x_plane[r:P:32, :].bitcast(I32), picked_rows[8 * r : P : 32, :].bitcast(I32))
+
+        picked_start = [64, table_start + T - 64]
+        picked = [
+            shared.tile([P, CHUNK], U32, name=f"picked{c}", align_bytes=64, offset=picked_start[c])
+            for c in range(S // CHUNK)
+        ]
+        codes = [
+            shared.tile([P, N], U32, name=f"codes{i}", align_bytes=64, offset=table_start + 4 * N * (i + 1))
+            for i in range(3)
+        ]
+        planes = [held.tile([P, N], U8, name=f"plane{i}", align_bytes=64) for i in range(3)]
+        banks = [[psum.tile([P, CHUNK], F32, name=f"bank{c}{i}") for i in range(3)] for c in range(S // CHUNK)]
+
+        def gather(c):
+            cols = CHUNK // 16
+            nc.vector.tensor_copy(picked[c][:], word_table[:].indirect(offsets[:, c * cols : (c + 1) * cols]))
+
+        def quantise(i):
+            grouped = held.tile([P, N, PACK], BF16, name=f"grouped{i}", align_bytes=64)
+            nc.scalar.copy(
+                grouped[:].rearrange("p (c j) t -> p c t j", j=4),
+                raw[i][:].rearrange("p t (c j) -> p c t j", j=4),
+            )
+            nc.vector.quantize_mx(
+                out=codes[i][:].bitcast(FP8X4),
+                scales=planes[i][:],
+                in_=grouped[:].rearrange("p n t -> p (n t)"),
+            )
+
+        def product(c, i):
+            nc.tensor.matmul_mx(
+                out=banks[c][i][:],
+                lhsT=codes[i][:].bitcast(FP8X4),
+                lhsT_scale=planes[i][:],
+                rhs=picked[c][:].bitcast(FP8X4),
+                rhs_scale=x_plane[:, c * CHUNK : (c + 1) * CHUNK],
+                start=True,
+                stop=True,
+            )
+
+        def finish(c):
+            pieces = [slice(h * PIECE, (h + 1) * PIECE) for h in range(CHUNK // PIECE)]
+            first = [held.tile([P, PIECE], F32, name=f"first{c}{h}") for h in range(len(pieces))]
+            second = [held.tile([P, PIECE], F32, name=f"second{c}{h}") for h in range(len(pieces))]
+            third = [held.tile([P, PIECE], F32, name=f"third{c}{h}") for h in range(len(pieces))]
+            for h, cols in enumerate(pieces):
+                nc.scalar.copy(first[h][:], banks[c][0][:, cols])
+            for h, cols in enumerate(pieces):
+                nc.vector.tensor_tensor(second[h][:], banks[c][1][:, cols], first[h][:], MAX)
+            for h, cols in enumerate(pieces):
+                nc.vector.tensor_tensor(third[h][:], banks[c][2][:, cols], second[h][:], MAX)
+                start = c * CHUNK + h * PIECE
+                nc.sync.dma_start(out[:, start : start + PIECE], third[h][:])
+
+        quantise(0)
+        gather(0)
+        product(0, 0)
+        quantise(1)
+        product(0, 1)
+        gather(1)
+        product(1, 0)
+        quantise(2)
+        product(0, 2)
+        product(1, 1)
+        product(1, 2)
+        finish(0)
+        finish(1)

@@ -16,6 +16,7 @@ P = 128
 PACK = 4
 CHUNK = 512
 PIECE = 256
+LEAD = 640
 
 
 def tile_picked_maxout_max_p_kernel(tc, x_words, x_scales, w1, w2, w3, offs, out):
@@ -23,52 +24,53 @@ def tile_picked_maxout_max_p_kernel(tc, x_words, x_scales, w1, w2, w3, offs, out
     with (
         tc.tile_pool(name="held", bufs=1) as held,
         tc.tile_pool(name="shared", bufs=1) as shared,
+        tc.tile_pool(name="spent", bufs=1) as spent,
         tc.psum_pool(name="psum", bufs=1) as psum,
     ):
+        word_table = held.tile([P, T], U32, name="word_table", align_bytes=64)
+        words = x_words[0].rearrange("p c t -> p (c t)").bitcast(I32)
+
+        def load_words(cols):
+            nc.sync.dma_start(word_table[:, cols].bitcast(I32), words[:, cols])
+
+        raw = [
+            held.tile([P, PACK, N], F32, name="raw0", align_bytes=64),
+            held.tile([P, PACK, N], F32, name="raw1", align_bytes=64),
+        ]
+        rows = [w.rearrange("(p t) n -> p t n", t=PACK) for w in (w1, w2, w3)]
         offsets = held.tile([P, S // 16], U16, name="offsets")
+        nc.sync.dma_start(raw[0][:], rows[0])
+        load_words(slice(0, LEAD))
         nc.sync.dma_start(offsets[:], offs)
 
-        word_table = held.tile([P, T], U32, name="word_table", align_bytes=64)
-        raw = [held.tile([P, PACK, N], F32, name=f"raw{i}", align_bytes=64) for i in range(3)]
-
-        def load_weight(i, w):
-            nc.scalar.dma_start(raw[i][:], w.rearrange("(p t) n -> p t n", t=PACK))
-
-        load_weight(0, w1)
-        nc.scalar.dma_start(word_table[:].bitcast(I32), x_words[0].rearrange("p c t -> p (c t)").bitcast(I32))
-        load_weight(1, w2)
-        load_weight(2, w3)
-
-        table_start = 4 * CHUNK
-        scale_table = shared.tile([P, T], U8, name="scale_table", align_bytes=64, offset=table_start)
+        scale_table = spent.tile([P, T], U8, name="scale_table", align_bytes=64, offset=0)
         nc.vector.memset(scale_table[:].bitcast(I32), 0)
         nc.sync.dma_start(scale_table[0:P:8, :].bitcast(I32), x_scales[0].bitcast(I32))
+        load_words(slice(LEAD, T))
+        nc.sync.dma_start(raw[1][:], rows[1])
+
         x_plane = held.tile([P, S], U8, name="x_plane", align_bytes=64)
         nc.vector.memset(x_plane[:].bitcast(I32), 0)
-
         picked_rows = held.tile([P, S], U8, name="picked_rows", align_bytes=64)
         nc.vector.tensor_copy(picked_rows[:], scale_table[:].indirect(offsets[:]))
         for r in range(4):
-            nc.sync.dma_start(x_plane[r:P:32, :].bitcast(I32), picked_rows[8 * r : P : 32, :].bitcast(I32))
+            queue = nc.sync if r % 2 == 0 else nc.scalar
+            queue.dma_start(x_plane[r:P:32, :].bitcast(I32), picked_rows[8 * r : P : 32, :].bitcast(I32))
+        raw.append(spent.tile([P, PACK, N], F32, name="raw2", align_bytes=64, offset=2048))
+        nc.sync.dma_start(raw[2][:], rows[2])
 
-        picked_start = [64, table_start + T - 64]
-        picked = [
-            shared.tile([P, CHUNK], U32, name=f"picked{c}", align_bytes=64, offset=picked_start[c])
-            for c in range(S // CHUNK)
-        ]
         codes = [
-            shared.tile([P, N], U32, name=f"codes{i}", align_bytes=64, offset=table_start + 4 * N * (i + 1))
-            for i in range(3)
+            spent.tile([P, N], U32, name="codes0", align_bytes=64, offset=0),
+            held.tile([P, N], U32, name="codes1", align_bytes=64),
+            held.tile([P, N], U32, name="codes2", align_bytes=64),
         ]
         planes = [held.tile([P, N], U8, name=f"plane{i}", align_bytes=64) for i in range(3)]
-        banks = [[psum.tile([P, CHUNK], F32, name=f"bank{c}{i}") for i in range(3)] for c in range(S // CHUNK)]
 
-        def gather(c):
+        def gather(c, picked):
             cols = CHUNK // 16
-            nc.vector.tensor_copy(picked[c][:], word_table[:].indirect(offsets[:, c * cols : (c + 1) * cols]))
+            nc.vector.tensor_copy(picked[:], word_table[:].indirect(offsets[:, c * cols : (c + 1) * cols]))
 
-        def quantise(i):
-            grouped = held.tile([P, N, PACK], BF16, name=f"grouped{i}", align_bytes=64)
+        def quantise(i, grouped):
             nc.scalar.copy(
                 grouped[:].rearrange("p (c j) t -> p c t j", j=4),
                 raw[i][:].rearrange("p t (c j) -> p c t j", j=4),
@@ -79,41 +81,52 @@ def tile_picked_maxout_max_p_kernel(tc, x_words, x_scales, w1, w2, w3, offs, out
                 in_=grouped[:].rearrange("p n t -> p (n t)"),
             )
 
-        def product(c, i):
-            nc.tensor.matmul_mx(
-                out=banks[c][i][:],
-                lhsT=codes[i][:].bitcast(FP8X4),
-                lhsT_scale=planes[i][:],
-                rhs=picked[c][:].bitcast(FP8X4),
-                rhs_scale=x_plane[:, c * CHUNK : (c + 1) * CHUNK],
-                start=True,
-                stop=True,
-            )
+        sums = {}
 
-        def finish(c):
-            pieces = [slice(h * PIECE, (h + 1) * PIECE) for h in range(CHUNK // PIECE)]
-            first = [held.tile([P, PIECE], F32, name=f"first{c}{h}") for h in range(len(pieces))]
-            second = [held.tile([P, PIECE], F32, name=f"second{c}{h}") for h in range(len(pieces))]
-            third = [held.tile([P, PIECE], F32, name=f"third{c}{h}") for h in range(len(pieces))]
-            for h, cols in enumerate(pieces):
-                nc.scalar.copy(first[h][:], banks[c][0][:, cols])
-            for h, cols in enumerate(pieces):
-                nc.vector.tensor_tensor(second[h][:], banks[c][1][:, cols], first[h][:], MAX)
-            for h, cols in enumerate(pieces):
-                nc.vector.tensor_tensor(third[h][:], banks[c][2][:, cols], second[h][:], MAX)
-                start = c * CHUNK + h * PIECE
-                nc.sync.dma_start(out[:, start : start + PIECE], third[h][:])
+        def product(i, c, picked, width):
+            for start in range(0, CHUNK, width):
+                bank = psum.tile([P, width], F32, name=f"bank{i}_{c}_{start}")
+                nc.tensor.matmul_mx(
+                    out=bank[:],
+                    lhsT=codes[i][:].bitcast(FP8X4),
+                    lhsT_scale=planes[i][:],
+                    rhs=picked[:, start : start + width].bitcast(FP8X4),
+                    rhs_scale=x_plane[:, c * CHUNK + start : c * CHUNK + start + width],
+                    start=True,
+                    stop=True,
+                )
+                for h in range(width // PIECE):
+                    sums[i, (c * CHUNK + start) // PIECE + h] = bank[:, h * PIECE : (h + 1) * PIECE]
 
-        quantise(0)
-        gather(0)
-        product(0, 0)
-        quantise(1)
-        product(0, 1)
-        gather(1)
-        product(1, 0)
-        quantise(2)
-        product(0, 2)
-        product(1, 1)
-        product(1, 2)
-        finish(0)
-        finish(1)
+        grouped0 = held.tile([P, N, PACK], BF16, name="grouped0", align_bytes=64)
+        quantise(0, grouped0)
+        picked0 = held.tile([P, CHUNK], U32, name="picked0", align_bytes=64)
+        gather(0, picked0)
+        product(0, 0, picked0, 512)
+        grouped1 = shared.tile([P, N, PACK], BF16, name="grouped1", tag="turn", align_bytes=64)
+        quantise(1, grouped1)
+        product(1, 0, picked0, 512)
+        picked1 = shared.tile([P, CHUNK], U32, name="picked1", tag="turn", align_bytes=64)
+        gather(1, picked1)
+        grouped2 = held.tile([P, N, PACK], BF16, name="grouped2", align_bytes=64)
+        quantise(2, grouped2)
+        product(0, 1, picked1, 512)
+        product(1, 1, picked1, 256)
+        product(2, 0, picked0, 256)
+        product(2, 1, picked1, 512)
+
+        pieces = range(S // PIECE)
+        copied = [
+            spent.tile([P, CHUNK], F32, name=f"copied{c}", align_bytes=64, offset=512 + 2048 * c) for c in range(2)
+        ]
+        first = [copied[h // 2][:, (h % 2) * PIECE : (h % 2 + 1) * PIECE] for h in pieces]
+        second = [held.tile([P, PIECE], F32, name=f"second{h}") for h in pieces]
+        third = [held.tile([P, PIECE], F32, name=f"third{h}") for h in pieces]
+        for h in pieces:
+            nc.scalar.copy(first[h], sums[0, h])
+        for h in pieces:
+            nc.vector.tensor_tensor(second[h][:], sums[1, h], first[h], MAX)
+        for h in pieces:
+            nc.vector.tensor_tensor(third[h][:], sums[2, h], second[h][:], MAX)
+            queue = nc.sync if h % 2 == 0 else nc.scalar
+            queue.dma_start(out[:, h * PIECE : (h + 1) * PIECE], third[h][:])

@@ -48,6 +48,8 @@ def tile_picked_maxout_max_p_kernel(tc, x_words, x_scales, w1, w2, w3, offs, out
         nc.sync.dma_start(scale_table[0:P:8, :].bitcast(I32), x_scales[0].bitcast(I32))
         load_words(slice(LEAD, T))
         nc.sync.dma_start(raw[1][:], rows[1])
+        raw.append(spent.tile([P, PACK, N], F32, name="raw2", align_bytes=64, offset=5120))
+        nc.sync.dma_start(raw[2][:], rows[2])
 
         x_plane = held.tile([P, S], U8, name="x_plane", align_bytes=64)
         nc.vector.memset(x_plane[:].bitcast(I32), 0)
@@ -56,8 +58,6 @@ def tile_picked_maxout_max_p_kernel(tc, x_words, x_scales, w1, w2, w3, offs, out
         for r in range(4):
             queue = nc.sync if r % 2 == 0 else nc.scalar
             queue.dma_start(x_plane[r:P:32, :].bitcast(I32), picked_rows[8 * r : P : 32, :].bitcast(I32))
-        raw.append(spent.tile([P, PACK, N], F32, name="raw2", align_bytes=64, offset=2048))
-        nc.sync.dma_start(raw[2][:], rows[2])
 
         codes = [
             spent.tile([P, N], U32, name="codes0", align_bytes=64, offset=0),
@@ -81,11 +81,10 @@ def tile_picked_maxout_max_p_kernel(tc, x_words, x_scales, w1, w2, w3, offs, out
                 in_=grouped[:].rearrange("p n t -> p (n t)"),
             )
 
-        sums = {}
-
         def product(i, c, picked, width):
+            sums = []
             for start in range(0, CHUNK, width):
-                bank = psum.tile([P, width], F32, name=f"bank{i}_{c}_{start}")
+                bank = psum.tile([P, width], F32, name=f"bank{i}_{start}", bufs=2 if i == 0 else 1)
                 nc.tensor.matmul_mx(
                     out=bank[:],
                     lhsT=codes[i][:].bitcast(FP8X4),
@@ -95,38 +94,48 @@ def tile_picked_maxout_max_p_kernel(tc, x_words, x_scales, w1, w2, w3, offs, out
                     start=True,
                     stop=True,
                 )
-                for h in range(width // PIECE):
-                    sums[i, (c * CHUNK + start) // PIECE + h] = bank[:, h * PIECE : (h + 1) * PIECE]
+                sums.extend(bank[:, h * PIECE : (h + 1) * PIECE] for h in range(width // PIECE))
+            return sums
+
+        def finish(c, sums):
+            copied = spent.tile([P, CHUNK], F32, name=f"copied{c}", align_bytes=64, offset=4096 + 2048 * c)
+            halves = range(CHUNK // PIECE)
+            larger = [held.tile([P, PIECE], F32, name=f"larger{c}_{h}") for h in halves]
+            largest = [held.tile([P, PIECE], F32, name=f"largest{c}_{h}") for h in halves]
+            for h in halves:
+                nc.scalar.copy(copied[:, h * PIECE : (h + 1) * PIECE], sums[0][h])
+            for h in halves:
+                nc.vector.tensor_tensor(larger[h][:], sums[1][h], copied[:, h * PIECE : (h + 1) * PIECE], MAX)
+            for h in halves:
+                nc.vector.tensor_tensor(largest[h][:], sums[2][h], larger[h][:], MAX)
+                start = c * CHUNK + h * PIECE
+                queue = nc.scalar if start + PIECE == S else nc.sync
+                queue.dma_start(out[:, start : start + PIECE], largest[h][:])
 
         grouped0 = held.tile([P, N, PACK], BF16, name="grouped0", align_bytes=64)
         quantise(0, grouped0)
+        spare = psum.tile([P, CHUNK], F32, name="spare")
+        for n in range(18):
+            nc.tensor.matmul_mx(
+                out=spare[0:32, (n % 4) * N : (n % 4 + 1) * N],
+                lhsT=codes[0][:, 0:32].bitcast(FP8X4),
+                lhsT_scale=planes[0][:, 0:32],
+                rhs=codes[0][:].bitcast(FP8X4),
+                rhs_scale=planes[0][:],
+                start=True,
+                stop=True,
+            )
         picked0 = held.tile([P, CHUNK], U32, name="picked0", align_bytes=64)
         gather(0, picked0)
-        product(0, 0, picked0, 512)
+        sums = [product(0, 0, picked0, CHUNK)]
         grouped1 = shared.tile([P, N, PACK], BF16, name="grouped1", tag="turn", align_bytes=64)
         quantise(1, grouped1)
-        product(1, 0, picked0, 512)
+        sums.append(product(1, 0, picked0, CHUNK))
         picked1 = shared.tile([P, CHUNK], U32, name="picked1", tag="turn", align_bytes=64)
         gather(1, picked1)
+        later = [product(0, 1, picked1, CHUNK)]
         grouped2 = held.tile([P, N, PACK], BF16, name="grouped2", align_bytes=64)
         quantise(2, grouped2)
-        product(0, 1, picked1, 512)
-        product(1, 1, picked1, 256)
-        product(2, 0, picked0, 256)
-        product(2, 1, picked1, 512)
-
-        pieces = range(S // PIECE)
-        copied = [
-            spent.tile([P, CHUNK], F32, name=f"copied{c}", align_bytes=64, offset=512 + 2048 * c) for c in range(2)
-        ]
-        first = [copied[h // 2][:, (h % 2) * PIECE : (h % 2 + 1) * PIECE] for h in pieces]
-        second = [held.tile([P, PIECE], F32, name=f"second{h}") for h in pieces]
-        third = [held.tile([P, PIECE], F32, name=f"third{h}") for h in pieces]
-        for h in pieces:
-            nc.scalar.copy(first[h], sums[0, h])
-        for h in pieces:
-            nc.vector.tensor_tensor(second[h][:], sums[1, h], first[h], MAX)
-        for h in pieces:
-            nc.vector.tensor_tensor(third[h][:], sums[2, h], second[h][:], MAX)
-            queue = nc.sync if h % 2 == 0 else nc.scalar
-            queue.dma_start(out[:, h * PIECE : (h + 1) * PIECE], third[h][:])
+        sums.append(product(2, 0, picked0, PIECE))
+        finish(0, sums)
+        finish(1, later + [product(1, 1, picked1, CHUNK), product(2, 1, picked1, PIECE)])

@@ -16,14 +16,12 @@ P = 128
 PACK = 4
 CHUNK = 512
 PIECE = 256
-LEAD = 640
 
 
 def tile_picked_maxout_max_p_kernel(tc, x_words, x_scales, w1, w2, w3, offs, out):
     nc = tc.nc
     with (
         tc.tile_pool(name="held", bufs=1) as held,
-        tc.tile_pool(name="shared", bufs=1) as shared,
         tc.tile_pool(name="spent", bufs=1) as spent,
         tc.psum_pool(name="psum", bufs=1) as psum,
     ):
@@ -35,21 +33,17 @@ def tile_picked_maxout_max_p_kernel(tc, x_words, x_scales, w1, w2, w3, offs, out
 
         raw = [
             held.tile([P, PACK, N], F32, name="raw0", align_bytes=64),
-            held.tile([P, PACK, N], F32, name="raw1", align_bytes=64),
+            spent.tile([P, PACK, N], F32, name="raw1", align_bytes=64, offset=8192),
         ]
         rows = [w.rearrange("(p t) n -> p t n", t=PACK) for w in (w1, w2, w3)]
         offsets = held.tile([P, S // 16], U16, name="offsets")
-        nc.sync.dma_start(raw[0][:], rows[0])
-        load_words(slice(0, LEAD))
-        nc.sync.dma_start(offsets[:], offs)
-
         scale_table = spent.tile([P, T], U8, name="scale_table", align_bytes=64, offset=0)
-        nc.vector.memset(scale_table[:].bitcast(I32), 0)
-        nc.sync.dma_start(scale_table[0:P:8, :].bitcast(I32), x_scales[0].bitcast(I32))
-        load_words(slice(LEAD, T))
+        nc.sync.dma_start(scale_table[P - 16 :, :].bitcast(I32), x_scales[0].bitcast(I32))
+        nc.vector.memset(scale_table[: P - 16, :].bitcast(I32), 0)
+        nc.sync.dma_start(offsets[:], offs)
+        nc.sync.dma_start(raw[0][:], rows[0])
+        load_words(slice(0, T))
         nc.sync.dma_start(raw[1][:], rows[1])
-        raw.append(spent.tile([P, PACK, N], F32, name="raw2", align_bytes=64, offset=5120))
-        nc.sync.dma_start(raw[2][:], rows[2])
 
         x_plane = held.tile([P, S], U8, name="x_plane", align_bytes=64)
         nc.vector.memset(x_plane[:].bitcast(I32), 0)
@@ -57,14 +51,18 @@ def tile_picked_maxout_max_p_kernel(tc, x_words, x_scales, w1, w2, w3, offs, out
         nc.vector.tensor_copy(picked_rows[:], scale_table[:].indirect(offsets[:]))
         for r in range(4):
             queue = nc.sync if r % 2 == 0 else nc.scalar
-            queue.dma_start(x_plane[r:P:32, :].bitcast(I32), picked_rows[8 * r : P : 32, :].bitcast(I32))
+            queue.dma_start(x_plane[r:P:32, :].bitcast(I32), picked_rows[P - 16 + r : P : 4, :].bitcast(I32))
+        raw.append(spent.tile([P, PACK, N], F32, name="raw2", align_bytes=64, offset=3072))
+        nc.sync.dma_start(raw[2][:], rows[2])
 
         codes = [
-            spent.tile([P, N], U32, name="codes0", align_bytes=64, offset=0),
+            held.tile([P, CHUNK], U32, name="codes0", align_bytes=64),
             held.tile([P, N], U32, name="codes1", align_bytes=64),
             held.tile([P, N], U32, name="codes2", align_bytes=64),
         ]
-        planes = [held.tile([P, N], U8, name=f"plane{i}", align_bytes=64) for i in range(3)]
+        nc.vector.memset(codes[0][:, N:].bitcast(I32), 0)
+        planes = [spent.tile([P, N], U8, name="plane0", align_bytes=64, offset=0)]
+        planes += [held.tile([P, N], U8, name=f"plane{i}", align_bytes=64) for i in (1, 2)]
 
         def gather(c, picked):
             cols = CHUNK // 16
@@ -76,18 +74,20 @@ def tile_picked_maxout_max_p_kernel(tc, x_words, x_scales, w1, w2, w3, offs, out
                 raw[i][:].rearrange("p t (c j) -> p c t j", j=4),
             )
             nc.vector.quantize_mx(
-                out=codes[i][:].bitcast(FP8X4),
+                out=codes[i][:, :N].bitcast(FP8X4),
                 scales=planes[i][:],
                 in_=grouped[:].rearrange("p n t -> p (n t)"),
             )
 
+        banks = [0, 2, 1, 3, 4, 0, 5, 6, 7, 2, 1, 3]
+
         def product(i, c, picked, width):
             sums = []
             for start in range(0, CHUNK, width):
-                bank = psum.tile([P, width], F32, name=f"bank{i}_{start}", bufs=2 if i == 0 else 1)
+                bank = psum.tile([P, width], F32, name=f"bank{i}_{c}_{start}", tag=f"bank{banks.pop(0)}")
                 nc.tensor.matmul_mx(
                     out=bank[:],
-                    lhsT=codes[i][:].bitcast(FP8X4),
+                    lhsT=codes[i][:, :N].bitcast(FP8X4),
                     lhsT_scale=planes[i][:],
                     rhs=picked[:, start : start + width].bitcast(FP8X4),
                     rhs_scale=x_plane[:, c * CHUNK + start : c * CHUNK + start + width],
@@ -98,7 +98,7 @@ def tile_picked_maxout_max_p_kernel(tc, x_words, x_scales, w1, w2, w3, offs, out
             return sums
 
         def finish(c, sums):
-            copied = spent.tile([P, CHUNK], F32, name=f"copied{c}", align_bytes=64, offset=4096 + 2048 * c)
+            copied = spent.tile([P, CHUNK], F32, name=f"copied{c}", align_bytes=64, offset=2048 + 2048 * c)
             halves = range(CHUNK // PIECE)
             larger = [held.tile([P, PIECE], F32, name=f"larger{c}_{h}") for h in halves]
             largest = [held.tile([P, PIECE], F32, name=f"largest{c}_{h}") for h in halves]
@@ -114,28 +114,27 @@ def tile_picked_maxout_max_p_kernel(tc, x_words, x_scales, w1, w2, w3, offs, out
 
         grouped0 = held.tile([P, N, PACK], BF16, name="grouped0", align_bytes=64)
         quantise(0, grouped0)
-        spare = psum.tile([P, CHUNK], F32, name="spare")
-        for n in range(18):
-            nc.tensor.matmul_mx(
-                out=spare[0:32, (n % 4) * N : (n % 4 + 1) * N],
-                lhsT=codes[0][:, 0:32].bitcast(FP8X4),
-                lhsT_scale=planes[0][:, 0:32],
-                rhs=codes[0][:].bitcast(FP8X4),
-                rhs_scale=planes[0][:],
-                start=True,
-                stop=True,
-            )
+        spare = psum.tile([P, CHUNK], F32, name="spare", tag="bank7")
+        nc.tensor.matmul_mx(
+            out=spare[:],
+            lhsT=codes[0][:, :N].bitcast(FP8X4),
+            lhsT_scale=planes[0][:],
+            rhs=codes[0][:].bitcast(FP8X4),
+            rhs_scale=x_plane[:, :CHUNK],
+            start=True,
+            stop=True,
+        )
         picked0 = held.tile([P, CHUNK], U32, name="picked0", align_bytes=64)
         gather(0, picked0)
-        sums = [product(0, 0, picked0, CHUNK)]
-        grouped1 = shared.tile([P, N, PACK], BF16, name="grouped1", tag="turn", align_bytes=64)
+        sums = [product(0, 0, picked0, PIECE)]
+        grouped1 = held.tile([P, N, PACK], BF16, name="grouped1", align_bytes=64)
         quantise(1, grouped1)
-        sums.append(product(1, 0, picked0, CHUNK))
-        picked1 = shared.tile([P, CHUNK], U32, name="picked1", tag="turn", align_bytes=64)
+        sums.append(product(1, 0, picked0, PIECE))
+        picked1 = spent.tile([P, CHUNK], U32, name="picked1", align_bytes=64, offset=8192)
         gather(1, picked1)
-        later = [product(0, 1, picked1, CHUNK)]
+        later = [product(0, 1, picked1, PIECE)]
         grouped2 = held.tile([P, N, PACK], BF16, name="grouped2", align_bytes=64)
         quantise(2, grouped2)
         sums.append(product(2, 0, picked0, PIECE))
         finish(0, sums)
-        finish(1, later + [product(1, 1, picked1, CHUNK), product(2, 1, picked1, PIECE)])
+        finish(1, later + [product(1, 1, picked1, PIECE), product(2, 1, picked1, PIECE)])

@@ -56,11 +56,10 @@ def tile_picked_maxout_max_p_kernel(tc, x_words, x_scales, w1, w2, w3, offs, out
         nc.sync.dma_start(raw[2][:], rows[2])
 
         codes = [
-            held.tile([P, CHUNK], U32, name="codes0", align_bytes=64),
+            held.tile([P, N], U32, name="codes0", align_bytes=64),
             held.tile([P, N], U32, name="codes1", align_bytes=64),
             held.tile([P, N], U32, name="codes2", align_bytes=64),
         ]
-        nc.vector.memset(codes[0][:, N:].bitcast(I32), 0)
         planes = [spent.tile([P, N], U8, name="plane0", align_bytes=64, offset=0)]
         planes += [held.tile([P, N], U8, name=f"plane{i}", align_bytes=64) for i in (1, 2)]
 
@@ -114,16 +113,6 @@ def tile_picked_maxout_max_p_kernel(tc, x_words, x_scales, w1, w2, w3, offs, out
 
         grouped0 = held.tile([P, N, PACK], BF16, name="grouped0", align_bytes=64)
         quantise(0, grouped0)
-        spare = psum.tile([P, CHUNK], F32, name="spare", tag="bank7")
-        nc.tensor.matmul_mx(
-            out=spare[:],
-            lhsT=codes[0][:, :N].bitcast(FP8X4),
-            lhsT_scale=planes[0][:],
-            rhs=codes[0][:].bitcast(FP8X4),
-            rhs_scale=x_plane[:, :CHUNK],
-            start=True,
-            stop=True,
-        )
         picked0 = held.tile([P, CHUNK], U32, name="picked0", align_bytes=64)
         gather(0, picked0)
         sums = [product(0, 0, picked0, PIECE)]

@@ -50,8 +50,7 @@ def tile_picked_maxout_max_p_kernel(tc, x_words, x_scales, w1, w2, w3, offs, out
         picked_rows = held.tile([P, S], U8, name="picked_rows", align_bytes=64)
         nc.vector.tensor_copy(picked_rows[:], scale_table[:].indirect(offsets[:]))
         for r in range(4):
-            queue = nc.sync if r % 2 == 0 else nc.scalar
-            queue.dma_start(x_plane[r:P:32, :].bitcast(I32), picked_rows[P - 16 + r : P : 4, :].bitcast(I32))
+            nc.sync.dma_start(x_plane[r:P:32, :].bitcast(I32), picked_rows[P - 16 + r : P : 4, :].bitcast(I32))
         raw.append(spent.tile([P, PACK, N], F32, name="raw2", align_bytes=64, offset=3072))
         nc.sync.dma_start(raw[2][:], rows[2])
 

@@ -26,103 +26,112 @@ def tile_picked_maxout_max_p_kernel(tc, x_words, x_scales, w1, w2, w3, offs, out
         tc.psum_pool(name="psum", bufs=1) as psum,
     ):
         word_table = held.tile([P, T], U32, name="word_table", align_bytes=64)
-        words = x_words[0].rearrange("p c t -> p (c t)").bitcast(I32)
-
-        def load_words(cols):
-            nc.sync.dma_start(word_table[:, cols].bitcast(I32), words[:, cols])
-
-        raw = [
-            held.tile([P, PACK, N], F32, name="raw0", align_bytes=64),
-            spent.tile([P, PACK, N], F32, name="raw1", align_bytes=64, offset=8192),
-        ]
+        raw = [held.tile([P, PACK, N], F32, name=f"raw{i}", align_bytes=64) for i in range(3)]
         rows = [w.rearrange("(p t) n -> p t n", t=PACK) for w in (w1, w2, w3)]
         offsets = held.tile([P, S // 16], U16, name="offsets")
         scale_table = spent.tile([P, T], U8, name="scale_table", align_bytes=64, offset=0)
-        nc.sync.dma_start(scale_table[P - 16 :, :].bitcast(I32), x_scales[0].bitcast(I32))
-        nc.vector.memset(scale_table[: P - 16, :].bitcast(I32), 0)
-        nc.sync.dma_start(offsets[:], offs)
+        cleared = scale_table[:].bitcast(I32)
+        nc.vector.memset(cleared[:, :640], 0)
+        nc.gpsimd.memset(cleared[:, 640:], 0)
         nc.sync.dma_start(raw[0][:], rows[0])
-        load_words(slice(0, T))
         nc.sync.dma_start(raw[1][:], rows[1])
+        nc.sync.dma_start(offsets[:], offs)
+        nc.sync.dma_start(scale_table[32:96:4, :].bitcast(I32), x_scales[0].bitcast(I32))
+        nc.sync.dma_start(word_table[:].bitcast(I32), x_words[0].rearrange("p c t -> p (c t)").bitcast(I32))
+        nc.sync.dma_start(raw[2][:], rows[2])
 
         x_plane = held.tile([P, S], U8, name="x_plane", align_bytes=64)
         nc.vector.memset(x_plane[:].bitcast(I32), 0)
         picked_rows = held.tile([P, S], U8, name="picked_rows", align_bytes=64)
         nc.vector.tensor_copy(picked_rows[:], scale_table[:].indirect(offsets[:]))
         for r in range(4):
-            nc.sync.dma_start(x_plane[r:P:32, :].bitcast(I32), picked_rows[P - 16 + r : P : 4, :].bitcast(I32))
-        raw.append(spent.tile([P, PACK, N], F32, name="raw2", align_bytes=64, offset=3072))
-        nc.sync.dma_start(raw[2][:], rows[2])
+            nc.sync.dma_start(x_plane[r:P:32, :].bitcast(I32), picked_rows[32 + 4 * r : 96 : 16, :].bitcast(I32))
 
-        codes = [
-            held.tile([P, N], U32, name="codes0", align_bytes=64),
-            held.tile([P, N], U32, name="codes1", align_bytes=64),
-            held.tile([P, N], U32, name="codes2", align_bytes=64),
-        ]
-        planes = [spent.tile([P, N], U8, name="plane0", align_bytes=64, offset=0)]
-        planes += [held.tile([P, N], U8, name=f"plane{i}", align_bytes=64) for i in (1, 2)]
+        early = held.tile([P, 2 * N, PACK], BF16, name="early", align_bytes=64)
+        late = held.tile([P, N, PACK], BF16, name="late", align_bytes=64)
+        early_codes = held.tile([P, 2 * N], U32, name="early_codes", align_bytes=64)
+        late_codes = held.tile([P, N], U32, name="late_codes", align_bytes=64)
+        early_plane = spent.tile([P, 2 * N], U8, name="early_plane", align_bytes=64, offset=0)
+        late_plane = held.tile([P, N], U8, name="late_plane", align_bytes=64)
+        codes = [early_codes[:, :N], early_codes[:, N:], late_codes[:]]
+        planes = [early_plane[:, :N], early_plane[:, N:], late_plane[:]]
 
-        def gather(c, picked):
-            cols = CHUNK // 16
-            nc.vector.tensor_copy(picked[:], word_table[:].indirect(offsets[:, c * cols : (c + 1) * cols]))
-
-        def quantise(i, grouped):
+        def round_weight(i, grouped):
             nc.scalar.copy(
-                grouped[:].rearrange("p (c j) t -> p c t j", j=4),
+                grouped.rearrange("p (c j) t -> p c t j", j=4),
                 raw[i][:].rearrange("p t (c j) -> p c t j", j=4),
             )
+
+        def quantise(grouped, to_codes, to_plane):
             nc.vector.quantize_mx(
-                out=codes[i][:, :N].bitcast(FP8X4),
-                scales=planes[i][:],
-                in_=grouped[:].rearrange("p n t -> p (n t)"),
+                out=to_codes[:].bitcast(FP8X4), scales=to_plane[:], in_=grouped[:].rearrange("p n t -> p (n t)")
             )
 
-        banks = [0, 2, 1, 3, 4, 0, 5, 6, 7, 2, 1, 3]
+        round_weight(0, early[:, :N, :])
+        round_weight(1, early[:, N:, :])
+        quantise(early, early_codes, early_plane)
 
-        def product(i, c, picked, width):
-            sums = []
-            for start in range(0, CHUNK, width):
-                bank = psum.tile([P, width], F32, name=f"bank{i}_{c}_{start}", tag=f"bank{banks.pop(0)}")
-                nc.tensor.matmul_mx(
-                    out=bank[:],
-                    lhsT=codes[i][:, :N].bitcast(FP8X4),
-                    lhsT_scale=planes[i][:],
-                    rhs=picked[:, start : start + width].bitcast(FP8X4),
-                    rhs_scale=x_plane[:, c * CHUNK + start : c * CHUNK + start + width],
-                    start=True,
-                    stop=True,
-                )
-                sums.extend(bank[:, h * PIECE : (h + 1) * PIECE] for h in range(width // PIECE))
-            return sums
+        picked = [
+            spent.tile([P, CHUNK], U32, name="picked0", align_bytes=64, offset=256),
+            held.tile([P, CHUNK], U32, name="picked1", align_bytes=64),
+        ]
+        cols = CHUNK // 16
+        for c in range(2):
+            nc.vector.tensor_copy(picked[c][:], word_table[:].indirect(offsets[:, c * cols : (c + 1) * cols]))
+        round_weight(2, late[:])
+        quantise(late, late_codes, late_plane)
 
-        def finish(c, sums):
-            copied = spent.tile([P, CHUNK], F32, name=f"copied{c}", align_bytes=64, offset=2048 + 2048 * c)
-            halves = range(CHUNK // PIECE)
-            larger = [held.tile([P, PIECE], F32, name=f"larger{c}_{h}") for h in halves]
-            largest = [held.tile([P, PIECE], F32, name=f"largest{c}_{h}") for h in halves]
-            for h in halves:
-                nc.scalar.copy(copied[:, h * PIECE : (h + 1) * PIECE], sums[0][h])
-            for h in halves:
-                nc.vector.tensor_tensor(larger[h][:], sums[1][h], copied[:, h * PIECE : (h + 1) * PIECE], MAX)
-            for h in halves:
-                nc.vector.tensor_tensor(largest[h][:], sums[2][h], larger[h][:], MAX)
-                start = c * CHUNK + h * PIECE
-                queue = nc.scalar if start + PIECE == S else nc.sync
-                queue.dma_start(out[:, start : start + PIECE], largest[h][:])
+        sums = {}
 
-        grouped0 = held.tile([P, N, PACK], BF16, name="grouped0", align_bytes=64)
-        quantise(0, grouped0)
-        picked0 = held.tile([P, CHUNK], U32, name="picked0", align_bytes=64)
-        gather(0, picked0)
-        sums = [product(0, 0, picked0, PIECE)]
-        grouped1 = held.tile([P, N, PACK], BF16, name="grouped1", align_bytes=64)
-        quantise(1, grouped1)
-        sums.append(product(1, 0, picked0, PIECE))
-        picked1 = spent.tile([P, CHUNK], U32, name="picked1", align_bytes=64, offset=8192)
-        gather(1, picked1)
-        later = [product(0, 1, picked1, PIECE)]
-        grouped2 = held.tile([P, N, PACK], BF16, name="grouped2", align_bytes=64)
-        quantise(2, grouped2)
-        sums.append(product(2, 0, picked0, PIECE))
-        finish(0, sums)
-        finish(1, later + [product(1, 1, picked1, PIECE), product(2, 1, picked1, PIECE)])
+        def product(i, piece, bank):
+            c, start = divmod(piece * PIECE, CHUNK)
+            sums[i, piece] = psum.tile([P, PIECE], F32, name=f"sums{i}_{piece}", tag=f"bank{bank}")
+            nc.tensor.matmul_mx(
+                out=sums[i, piece][:],
+                lhsT=codes[i].bitcast(FP8X4),
+                lhsT_scale=planes[i],
+                rhs=picked[c][:, start : start + PIECE].bitcast(FP8X4),
+                rhs_scale=x_plane[:, piece * PIECE : (piece + 1) * PIECE],
+                start=True,
+                stop=True,
+            )
+
+        copied = [held.tile([P, PIECE], F32, name=f"copied{h}") for h in range(4)]
+        larger = [held.tile([P, PIECE], F32, name=f"larger{h}") for h in range(4)]
+        largest = [held.tile([P, PIECE], F32, name=f"largest{h}") for h in range(4)]
+
+        def copy(h):
+            nc.scalar.copy(copied[h][:], sums[0, h][:])
+
+        def first(h):
+            nc.vector.tensor_tensor(larger[h][:], sums[1, h][:], copied[h][:], MAX)
+
+        def second(h):
+            nc.vector.tensor_tensor(largest[h][:], sums[2, h][:], larger[h][:], MAX)
+            queue = nc.scalar if h == 3 else nc.sync
+            queue.dma_start(out[:, h * PIECE : (h + 1) * PIECE], largest[h][:])
+
+        product(0, 0, 0)
+        product(1, 0, 1)
+        product(0, 1, 2)
+        product(1, 1, 3)
+        copy(0)
+        copy(1)
+        product(0, 2, 4)
+        product(2, 0, 5)
+        product(2, 1, 6)
+        product(0, 3, 7)
+        product(1, 2, 0)
+        product(1, 3, 2)
+        copy(2)
+        copy(3)
+        first(0)
+        first(1)
+        product(2, 2, 1)
+        product(2, 3, 3)
+        second(0)
+        second(1)
+        first(2)
+        first(3)
+        second(2)
+        second(3)

@@ -14,8 +14,8 @@ MAX = mybir.AluOpType.max
 
 P = 128
 PACK = 4
-CHUNK = 512
 PIECE = 256
+PIECES = S // PIECE
 
 
 def tile_picked_maxout_max_p_kernel(tc, x_words, x_scales, w1, w2, w3, offs, out):
@@ -23,10 +23,13 @@ def tile_picked_maxout_max_p_kernel(tc, x_words, x_scales, w1, w2, w3, offs, out
     with (
         tc.tile_pool(name="held", bufs=1) as held,
         tc.tile_pool(name="spent", bufs=1) as spent,
+        tc.tile_pool(name="landing", bufs=1) as landing,
+        tc.tile_pool(name="rounded", bufs=1) as rounded,
         tc.psum_pool(name="psum", bufs=1) as psum,
     ):
         word_table = held.tile([P, T], U32, name="word_table", align_bytes=64)
-        raw = [held.tile([P, PACK, N], F32, name=f"raw{i}", align_bytes=64) for i in range(3)]
+        raw = [held.tile([P, PACK, N], F32, name=f"raw{i}", align_bytes=64) for i in range(2)]
+        raw.append(landing.tile([P, PACK, N], F32, name="raw2", align_bytes=64, offset=0))
         rows = [w.rearrange("(p t) n -> p t n", t=PACK) for w in (w1, w2, w3)]
         offsets = held.tile([P, S // 16], U16, name="offsets")
         scale_table = spent.tile([P, T], U8, name="scale_table", align_bytes=64, offset=0)
@@ -48,7 +51,7 @@ def tile_picked_maxout_max_p_kernel(tc, x_words, x_scales, w1, w2, w3, offs, out
             nc.sync.dma_start(x_plane[r:P:32, :].bitcast(I32), picked_rows[32 + 4 * r : 96 : 16, :].bitcast(I32))
 
         early = held.tile([P, 2 * N, PACK], BF16, name="early", align_bytes=64)
-        late = held.tile([P, N, PACK], BF16, name="late", align_bytes=64)
+        late = rounded.tile([P, N, PACK], BF16, name="late", align_bytes=64, offset=0)
         early_codes = held.tile([P, 2 * N], U32, name="early_codes", align_bytes=64)
         late_codes = held.tile([P, N], U32, name="late_codes", align_bytes=64)
         early_plane = spent.tile([P, 2 * N], U8, name="early_plane", align_bytes=64, offset=0)
@@ -71,67 +74,60 @@ def tile_picked_maxout_max_p_kernel(tc, x_words, x_scales, w1, w2, w3, offs, out
         round_weight(1, early[:, N:, :])
         quantise(early, early_codes, early_plane)
 
-        picked = [
-            spent.tile([P, CHUNK], U32, name="picked0", align_bytes=64, offset=256),
-            held.tile([P, CHUNK], U32, name="picked1", align_bytes=64),
+        halves = [
+            spent.tile([P, S // 2], U32, name="picked_early", align_bytes=64, offset=256),
+            landing.tile([P, S // 2], U32, name="picked_late", align_bytes=64, offset=0),
         ]
-        cols = CHUNK // 16
-        for c in range(2):
-            nc.vector.tensor_copy(picked[c][:], word_table[:].indirect(offsets[:, c * cols : (c + 1) * cols]))
+        picked = [halves[c // 2][:, c % 2 * PIECE : (c % 2 + 1) * PIECE] for c in range(PIECES)]
+        cols = PIECE // 16
+
+        def gather(c):
+            nc.vector.tensor_copy(picked[c], word_table[:].indirect(offsets[:, c * cols : (c + 1) * cols]))
+
+        gather(0)
+        gather(1)
         round_weight(2, late[:])
         quantise(late, late_codes, late_plane)
+        gather(2)
+        gather(3)
 
         sums = {}
 
-        def product(i, piece, bank):
-            c, start = divmod(piece * PIECE, CHUNK)
-            sums[i, piece] = psum.tile([P, PIECE], F32, name=f"sums{i}_{piece}", tag=f"bank{bank}")
+        def product(i, c):
+            bank = c + PIECES * (i == 1)
+            sums[i, c] = psum.tile([P, PIECE], F32, name=f"sums{i}_{c}", tag=f"bank{bank}")
             nc.tensor.matmul_mx(
-                out=sums[i, piece][:],
+                out=sums[i, c][:],
                 lhsT=codes[i].bitcast(FP8X4),
                 lhsT_scale=planes[i],
-                rhs=picked[c][:, start : start + PIECE].bitcast(FP8X4),
-                rhs_scale=x_plane[:, piece * PIECE : (piece + 1) * PIECE],
+                rhs=picked[c].bitcast(FP8X4),
+                rhs_scale=x_plane[:, c * PIECE : (c + 1) * PIECE],
                 start=True,
                 stop=True,
             )
 
-        copied = [held.tile([P, PIECE], F32, name=f"copied{h}") for h in range(4)]
-        larger = [held.tile([P, PIECE], F32, name=f"larger{h}") for h in range(4)]
-        largest = [held.tile([P, PIECE], F32, name=f"largest{h}") for h in range(4)]
+        first_sums = rounded.tile([P, S], F32, name="first_sums", align_bytes=64, offset=0)
+        copied = [first_sums[:, c * PIECE : (c + 1) * PIECE] for c in range(PIECES)]
+        larger = [held.tile([P, PIECE], F32, name=f"larger{c}") for c in range(PIECES)]
+        largest = [held.tile([P, PIECE], F32, name=f"largest{c}") for c in range(PIECES)]
 
-        def copy(h):
-            nc.scalar.copy(copied[h][:], sums[0, h][:])
+        def first(c):
+            nc.vector.tensor_tensor(larger[c][:], sums[1, c][:], copied[c], MAX)
 
-        def first(h):
-            nc.vector.tensor_tensor(larger[h][:], sums[1, h][:], copied[h][:], MAX)
+        def second(c):
+            nc.vector.tensor_tensor(largest[c][:], sums[2, c][:], larger[c][:], MAX)
+            queue = nc.scalar if c == PIECES - 1 else nc.sync
+            queue.dma_start(out[:, c * PIECE : (c + 1) * PIECE], largest[c][:])
 
-        def second(h):
-            nc.vector.tensor_tensor(largest[h][:], sums[2, h][:], larger[h][:], MAX)
-            queue = nc.scalar if h == 3 else nc.sync
-            queue.dma_start(out[:, h * PIECE : (h + 1) * PIECE], largest[h][:])
-
-        product(0, 0, 0)
-        product(1, 0, 1)
-        product(0, 1, 2)
-        product(1, 1, 3)
-        copy(0)
-        copy(1)
-        product(0, 2, 4)
-        product(2, 0, 5)
-        product(2, 1, 6)
-        product(0, 3, 7)
-        product(1, 2, 0)
-        product(1, 3, 2)
-        copy(2)
-        copy(3)
+        for c in range(PIECES):
+            product(0, c)
+            product(1, c)
+            nc.scalar.copy(copied[c], sums[0, c][:])
+            if c > 0:
+                product(2, c - 1)
+        product(2, PIECES - 1)
         first(0)
-        first(1)
-        product(2, 2, 1)
-        product(2, 3, 3)
-        second(0)
-        second(1)
-        first(2)
-        first(3)
-        second(2)
-        second(3)
+        for c in range(1, PIECES):
+            first(c)
+            second(c - 1)
+        second(PIECES - 1)

@@ -24,7 +24,6 @@ def tile_picked_maxout_max_p_kernel(tc, x_words, x_scales, w1, w2, w3, offs, out
         tc.tile_pool(name="held", bufs=1) as held,
         tc.tile_pool(name="spent", bufs=1) as spent,
         tc.tile_pool(name="landing", bufs=1) as landing,
-        tc.tile_pool(name="rounded", bufs=1) as rounded,
         tc.psum_pool(name="psum", bufs=1) as psum,
     ):
         word_table = held.tile([P, T], U32, name="word_table", align_bytes=64)
@@ -48,10 +47,11 @@ def tile_picked_maxout_max_p_kernel(tc, x_words, x_scales, w1, w2, w3, offs, out
         picked_rows = held.tile([P, S], U8, name="picked_rows", align_bytes=64)
         nc.vector.tensor_copy(picked_rows[:], scale_table[:].indirect(offsets[:]))
         for r in range(4):
-            nc.sync.dma_start(x_plane[r:P:32, :].bitcast(I32), picked_rows[32 + 4 * r : 96 : 16, :].bitcast(I32))
+            queue = nc.scalar if r % 2 else nc.sync
+            queue.dma_start(x_plane[r:P:32, :].bitcast(I32), picked_rows[32 + 4 * r : 96 : 16, :].bitcast(I32))
 
         early = held.tile([P, 2 * N, PACK], BF16, name="early", align_bytes=64)
-        late = rounded.tile([P, N, PACK], BF16, name="late", align_bytes=64, offset=0)
+        late = held.tile([P, N, PACK], BF16, name="late", align_bytes=64)
         early_codes = held.tile([P, 2 * N], U32, name="early_codes", align_bytes=64)
         late_codes = held.tile([P, N], U32, name="late_codes", align_bytes=64)
         early_plane = spent.tile([P, 2 * N], U8, name="early_plane", align_bytes=64, offset=0)
@@ -74,60 +74,69 @@ def tile_picked_maxout_max_p_kernel(tc, x_words, x_scales, w1, w2, w3, offs, out
         round_weight(1, early[:, N:, :])
         quantise(early, early_codes, early_plane)
 
-        halves = [
-            spent.tile([P, S // 2], U32, name="picked_early", align_bytes=64, offset=256),
-            landing.tile([P, S // 2], U32, name="picked_late", align_bytes=64, offset=0),
-        ]
-        picked = [halves[c // 2][:, c % 2 * PIECE : (c % 2 + 1) * PIECE] for c in range(PIECES)]
+        picked = [held.tile([P, PIECE], U32, name=f"picked{c}", align_bytes=64) for c in range(PIECES - 1)]
+        picked.append(landing.tile([P, PIECE], U32, name="picked_last", align_bytes=64, offset=0))
         cols = PIECE // 16
 
         def gather(c):
-            nc.vector.tensor_copy(picked[c], word_table[:].indirect(offsets[:, c * cols : (c + 1) * cols]))
+            nc.vector.tensor_copy(picked[c][:], word_table[:].indirect(offsets[:, c * cols : (c + 1) * cols]))
 
-        gather(0)
-        gather(1)
+        for c in range(PIECES - 1):
+            gather(c)
         round_weight(2, late[:])
         quantise(late, late_codes, late_plane)
-        gather(2)
-        gather(3)
+        gather(PIECES - 1)
 
         sums = {}
 
-        def product(i, c):
-            bank = c + PIECES * (i == 1)
+        def product(i, c, bank):
             sums[i, c] = psum.tile([P, PIECE], F32, name=f"sums{i}_{c}", tag=f"bank{bank}")
             nc.tensor.matmul_mx(
                 out=sums[i, c][:],
                 lhsT=codes[i].bitcast(FP8X4),
                 lhsT_scale=planes[i],
-                rhs=picked[c].bitcast(FP8X4),
+                rhs=picked[c][:].bitcast(FP8X4),
                 rhs_scale=x_plane[:, c * PIECE : (c + 1) * PIECE],
                 start=True,
                 stop=True,
             )
 
-        first_sums = rounded.tile([P, S], F32, name="first_sums", align_bytes=64, offset=0)
-        copied = [first_sums[:, c * PIECE : (c + 1) * PIECE] for c in range(PIECES)]
+        copied = [held.tile([P, PIECE], F32, name=f"copied{c}") for c in range(PIECES)]
         larger = [held.tile([P, PIECE], F32, name=f"larger{c}") for c in range(PIECES)]
         largest = [held.tile([P, PIECE], F32, name=f"largest{c}") for c in range(PIECES)]
 
+        def copy(c):
+            nc.scalar.copy(copied[c][:], sums[0, c][:])
+
         def first(c):
-            nc.vector.tensor_tensor(larger[c][:], sums[1, c][:], copied[c], MAX)
+            nc.vector.tensor_tensor(larger[c][:], sums[1, c][:], copied[c][:], MAX)
 
         def second(c):
             nc.vector.tensor_tensor(largest[c][:], sums[2, c][:], larger[c][:], MAX)
             queue = nc.scalar if c == PIECES - 1 else nc.sync
             queue.dma_start(out[:, c * PIECE : (c + 1) * PIECE], largest[c][:])
 
-        for c in range(PIECES):
-            product(0, c)
-            product(1, c)
-            nc.scalar.copy(copied[c], sums[0, c][:])
-            if c > 0:
-                product(2, c - 1)
-        product(2, PIECES - 1)
+        product(0, 0, 0)
+        product(1, 0, 1)
+        copy(0)
+        product(0, 1, 2)
+        product(1, 1, 3)
+        copy(1)
+        product(0, 2, 4)
+        product(2, 0, 5)
+        copy(2)
+        product(1, 2, 6)
+        product(0, 3, 7)
+        copy(3)
+        product(2, 1, 0)
+        product(1, 3, 2)
         first(0)
-        for c in range(1, PIECES):
-            first(c)
-            second(c - 1)
-        second(PIECES - 1)
+        first(1)
+        product(2, 2, 1)
+        product(2, 3, 3)
+        second(0)
+        first(2)
+        second(1)
+        first(3)
+        second(2)
+        second(3)

@@ -32,9 +32,7 @@ def tile_picked_maxout_max_p_kernel(tc, x_words, x_scales, w1, w2, w3, offs, out
         rows = [w.rearrange("(p t) n -> p t n", t=PACK) for w in (w1, w2, w3)]
         offsets = held.tile([P, S // 16], U16, name="offsets")
         scale_table = spent.tile([P, T], U8, name="scale_table", align_bytes=64, offset=0)
-        cleared = scale_table[:].bitcast(I32)
-        nc.vector.memset(cleared[:, :640], 0)
-        nc.gpsimd.memset(cleared[:, 640:], 0)
+        nc.vector.memset(scale_table[:].bitcast(I32), 0)
         nc.sync.dma_start(raw[0][:], rows[0])
         nc.sync.dma_start(raw[1][:], rows[1])
         nc.sync.dma_start(offsets[:], offs)

@@ -114,11 +114,11 @@ def tile_picked_maxout_max_p_kernel(tc, x_words, x_scales, w1, w2, w3, offs, out
             queue = nc.scalar if c == PIECES - 1 else nc.sync
             queue.dma_start(out[:, c * PIECE : (c + 1) * PIECE], largest[c][:])
 
-        product(0, 0, 0)
         product(1, 0, 1)
+        product(0, 0, 0)
         copy(0)
-        product(0, 1, 2)
         product(1, 1, 3)
+        product(0, 1, 2)
         copy(1)
         product(0, 2, 4)
         product(2, 0, 5)

@@ -16,6 +16,7 @@ P = 128
 PACK = 4
 PIECE = 256
 PIECES = S // PIECE
+SPLIT = 80
 
 
 def tile_picked_maxout_max_p_kernel(tc, x_words, x_scales, w1, w2, w3, offs, out):
@@ -81,7 +82,11 @@ def tile_picked_maxout_max_p_kernel(tc, x_words, x_scales, w1, w2, w3, offs, out
 
         for c in range(PIECES - 1):
             gather(c)
-        round_weight(2, late[:])
+        nc.scalar.copy(
+            late[:, :SPLIT, :].rearrange("p (c j) t -> p c t j", j=4),
+            raw[2][:, :, :SPLIT].rearrange("p t (c j) -> p c t j", j=4),
+        )
+        nc.gpsimd.tensor_copy(late[:, SPLIT:, :], raw[2][:, :, SPLIT:].rearrange("p t n -> p n t"))
         quantise(late, late_codes, late_plane)
         gather(PIECES - 1)
 

import concourse.mybir as mybir

K, T, S, N = 512, 4096, 1024, 128
FLOPS = 3 * 2 * K * N * S

F32 = mybir.dt.float32
BF16 = mybir.dt.bfloat16
I32 = mybir.dt.int32
U32 = mybir.dt.uint32
U16 = mybir.dt.uint16
U8 = mybir.dt.uint8
FP8X4 = mybir.dt.float8_e4m3fn_x4
MAX = mybir.AluOpType.max

P = 128
PACK = 4
PIECE = 256
PIECES = S // PIECE
SPLIT = 80


def tile_picked_maxout_max_p_kernel(tc, x_words, x_scales, w1, w2, w3, offs, out):
    nc = tc.nc
    with (
        tc.tile_pool(name="held", bufs=1) as held,
        tc.tile_pool(name="spent", bufs=1) as spent,
        tc.tile_pool(name="landing", bufs=1) as landing,
        tc.psum_pool(name="psum", bufs=1) as psum,
    ):
        word_table = held.tile([P, T], U32, name="word_table", align_bytes=64)
        raw = [held.tile([P, PACK, N], F32, name=f"raw{i}", align_bytes=64) for i in range(2)]
        raw.append(landing.tile([P, PACK, N], F32, name="raw2", align_bytes=64, offset=0))
        rows = [w.rearrange("(p t) n -> p t n", t=PACK) for w in (w1, w2, w3)]
        offsets = held.tile([P, S // 16], U16, name="offsets")
        scale_table = spent.tile([P, T], U8, name="scale_table", align_bytes=64, offset=0)
        nc.vector.memset(scale_table[:].bitcast(I32), 0)
        nc.sync.dma_start(raw[0][:], rows[0])
        nc.sync.dma_start(raw[1][:], rows[1])
        nc.sync.dma_start(offsets[:], offs)
        nc.sync.dma_start(scale_table[32:96:4, :].bitcast(I32), x_scales[0].bitcast(I32))
        nc.sync.dma_start(word_table[:].bitcast(I32), x_words[0].rearrange("p c t -> p (c t)").bitcast(I32))
        nc.sync.dma_start(raw[2][:], rows[2])

        x_plane = held.tile([P, S], U8, name="x_plane", align_bytes=64)
        nc.vector.memset(x_plane[:].bitcast(I32), 0)
        picked_rows = held.tile([P, S], U8, name="picked_rows", align_bytes=64)
        nc.vector.tensor_copy(picked_rows[:], scale_table[:].indirect(offsets[:]))
        for r in range(4):
            queue = nc.scalar if r % 2 else nc.sync
            queue.dma_start(x_plane[r:P:32, :].bitcast(I32), picked_rows[32 + 4 * r : 96 : 16, :].bitcast(I32))

        early = held.tile([P, 2 * N, PACK], BF16, name="early", align_bytes=64)
        late = held.tile([P, N, PACK], BF16, name="late", align_bytes=64)
        early_codes = held.tile([P, 2 * N], U32, name="early_codes", align_bytes=64)
        late_codes = held.tile([P, N], U32, name="late_codes", align_bytes=64)
        early_plane = spent.tile([P, 2 * N], U8, name="early_plane", align_bytes=64, offset=0)
        late_plane = held.tile([P, N], U8, name="late_plane", align_bytes=64)
        codes = [early_codes[:, :N], early_codes[:, N:], late_codes[:]]
        planes = [early_plane[:, :N], early_plane[:, N:], late_plane[:]]

        def round_weight(i, grouped):
            nc.scalar.copy(
                grouped.rearrange("p (c j) t -> p c t j", j=4),
                raw[i][:].rearrange("p t (c j) -> p c t j", j=4),
            )

        def quantise(grouped, to_codes, to_plane):
            nc.vector.quantize_mx(
                out=to_codes[:].bitcast(FP8X4), scales=to_plane[:], in_=grouped[:].rearrange("p n t -> p (n t)")
            )

        round_weight(0, early[:, :N, :])
        round_weight(1, early[:, N:, :])
        quantise(early, early_codes, early_plane)

        picked = [held.tile([P, PIECE], U32, name=f"picked{c}", align_bytes=64) for c in range(PIECES - 1)]
        picked.append(landing.tile([P, PIECE], U32, name="picked_last", align_bytes=64, offset=0))
        cols = PIECE // 16

        def gather(c):
            nc.vector.tensor_copy(picked[c][:], word_table[:].indirect(offsets[:, c * cols : (c + 1) * cols]))

        for c in range(PIECES - 1):
            gather(c)
        nc.scalar.copy(
            late[:, :SPLIT, :].rearrange("p (c j) t -> p c t j", j=4),
            raw[2][:, :, :SPLIT].rearrange("p t (c j) -> p c t j", j=4),
        )
        nc.gpsimd.tensor_copy(late[:, SPLIT:, :], raw[2][:, :, SPLIT:].rearrange("p t n -> p n t"))
        quantise(late, late_codes, late_plane)
        gather(PIECES - 1)

        sums = {}

        def product(i, c, bank):
            sums[i, c] = psum.tile([P, PIECE], F32, name=f"sums{i}_{c}", tag=f"bank{bank}")
            nc.tensor.matmul_mx(
                out=sums[i, c][:],
                lhsT=codes[i].bitcast(FP8X4),
                lhsT_scale=planes[i],
                rhs=picked[c][:].bitcast(FP8X4),
                rhs_scale=x_plane[:, c * PIECE : (c + 1) * PIECE],
                start=True,
                stop=True,
            )

        copied = [held.tile([P, PIECE], F32, name=f"copied{c}") for c in range(PIECES)]
        larger = [held.tile([P, PIECE], F32, name=f"larger{c}") for c in range(PIECES)]
        largest = [held.tile([P, PIECE], F32, name=f"largest{c}") for c in range(PIECES)]

        def copy(c):
            nc.scalar.copy(copied[c][:], sums[0, c][:])

        def first(c):
            nc.vector.tensor_tensor(larger[c][:], sums[1, c][:], copied[c][:], MAX)

        def second(c):
            nc.vector.tensor_tensor(largest[c][:], sums[2, c][:], larger[c][:], MAX)
            queue = nc.scalar if c == PIECES - 1 else nc.sync
            queue.dma_start(out[:, c * PIECE : (c + 1) * PIECE], largest[c][:])

        product(1, 0, 1)
        product(0, 0, 0)
        copy(0)
        product(1, 1, 3)
        product(0, 1, 2)
        copy(1)
        product(0, 2, 4)
        product(2, 0, 5)
        copy(2)
        product(1, 2, 6)
        product(0, 3, 7)
        copy(3)
        product(2, 1, 0)
        product(1, 3, 2)
        first(0)
        first(1)
        product(2, 2, 1)
        product(2, 3, 3)
        second(0)
        first(2)
        second(1)
        first(3)
        second(2)
        second(3)
